import numpy as np
import ml_dtypes


def mxq(x, axis, fmt="e4m3"):
    dtype, down = {"e4m3": (ml_dtypes.float8_e4m3fn, 7), "e5m2": (ml_dtypes.float8_e5m2, 14)}[fmt]
    v = np.moveaxis(np.asarray(x, np.float32).astype(ml_dtypes.bfloat16).astype(np.float64), axis, -1)
    blocks = v.reshape(v.shape[:-1] + (-1, 32))
    amax = np.abs(blocks).max(-1, keepdims=True)
    byte = np.maximum(np.where(amax > 0, np.frexp(amax)[1] - 1 + 127, 0) - down, 1)
    scale = np.exp2(byte - 127.0)
    codes = (blocks / scale).astype(np.float32).astype(dtype).astype(np.float64)
    return np.moveaxis((codes * scale).reshape(v.shape), -1, axis)


WIDE = False


def mx_kscale(k):
    if not WIDE:
        return np.ones(k)
    levels = np.array([10, -10, 5, -5, 0])
    if k % 512:
        return np.exp2(np.random.permutation(np.resize(levels, k // 32))).repeat(32)
    a = np.empty((k // 512, 16))
    for p in range(k // 512):
        a[p, :8] = np.random.permutation(np.resize(levels, 8))
        for g in range(8):
            far = levels[np.abs(levels - a[p, g]) >= 10]
            a[p, g + 8] = far[np.random.randint(len(far))]
    return np.exp2(a.ravel()).repeat(32)


def f64(x):
    return np.asarray(x).astype(np.float64)


def striped(idx):
    return np.tile(idx.reshape(-1, 16).T, (8, 1)).astype(np.uint16)


def unstriped(offs):
    return offs[:16].T.reshape(-1).astype(np.int64)


E2M1 = np.array([0.0, 0.5, 1.0, 1.5, 2.0, 3.0, 4.0, 6.0, -0.0, -0.5, -1.0, -1.5, -2.0, -3.0, -4.0, -6.0])


def pack_weight(w, fmt):
    k, n = w.shape
    w = f64(np.asarray(w, np.float32).astype(ml_dtypes.bfloat16)).reshape(k // 32, 32, n)
    amax = np.abs(w).max(1)
    if fmt == "e4m3":
        byte = np.frexp(amax)[1] - 1 + 127 - 7
    else:
        mant, ex = np.frexp(amax / 6.0)
        byte = np.where(mant > 0.5, ex, ex - 1) + 127
    byte = np.clip(np.where(amax > 0, byte, 1), 1, 254)
    scaled = (w * np.exp2(127.0 - byte)[:, None, :]).reshape(k, n).astype(np.float32)
    by_word = np.ascontiguousarray(scaled.reshape(k // 512, 128, 4, n).transpose(0, 1, 3, 2))
    if fmt == "e4m3":
        words = by_word.astype(ml_dtypes.float8_e4m3fn).view(np.uint8)
    else:
        c = by_word.astype(ml_dtypes.float4_e2m1fn).view(np.uint8) & 0xF
        words = (c[..., 0::2] | (c[..., 1::2] << 4)).reshape(k // 512, 128, 2 * n)
    return np.ascontiguousarray(words), np.ascontiguousarray(byte.astype(np.uint8).reshape(k // 512, 16, n))


def unpack_weight(words, scales, fmt):
    g, _, n = scales.shape
    words = np.ascontiguousarray(words).reshape(g, 128, n, -1)
    if fmt == "e4m3":
        vals = words.view(ml_dtypes.float8_e4m3fn).astype(np.float64)
    else:
        nib = np.empty((g, 128, n, 4), np.uint8)
        nib[..., 0::2] = words & 0xF
        nib[..., 1::2] = words >> 4
        vals = E2M1[nib]
    vals = vals * np.repeat(np.exp2(scales.astype(np.float64) - 127.0), 8, axis=1)[..., None]
    return vals.transpose(0, 1, 3, 2).reshape(g * 512, n)


def gelu(v):
    return 0.5 * v * (1.0 + np.tanh(np.sqrt(2.0 / np.pi) * (v + 0.044715 * v**3)))


def striped8(idx):
    return np.concatenate([v.reshape(-1, 16).T for v in idx]).astype(np.uint16)


def unstriped8(offs):
    return np.stack([offs[16 * g:16 * g + 16].T.reshape(-1) for g in range(8)]).astype(np.int64)


def runs(v, idx8):
    k = np.arange(v.shape[0])
    return v[k[:, None], idx8[k % 512 // 64]]


K, H, N, T, S, P = 1024, 1536, 384, 2048, 1024, 512


def setup_inputs():
    n = np.random.standard_normal
    s = mx_kscale(K)[:, None]
    u = mx_kscale(H)[:, None]
    d = {}
    d["tab_words"], d["tab_scales"] = pack_weight(n((K, T)) * s, "e4m3")
    d["offs"] = striped8(np.stack([np.random.permutation(T)[:S] for _ in range(8)]))
    d["w1"] = (1.5 * n((K, H)) / s / K ** 0.5).astype(np.float32)
    d["b1"] = (0.5 * n(H)).astype(np.float32)
    d["gain"] = (np.exp(0.3 * n(H)) * u[:, 0]).astype(np.float32)
    d["pos1"] = striped(np.random.permutation(S)[:P])
    d["pos2"] = striped(np.random.permutation(S)[:P])
    d["w2"] = (n((H, N)) / u / H ** 0.5).astype(np.float32)
    d["w3_words"], d["w3_scales"] = pack_weight(n((H, N)) / u / H ** 0.5, "e2m1")
    return d


def reference(tab_words, tab_scales, offs, w1, b1, gain, pos1, pos2, w2, w3_words, w3_scales):
    v = runs(unpack_weight(tab_words, tab_scales, "e4m3"), unstriped8(offs))
    lin = mxq(f64(w1), 0, "e4m3").T @ v
    h = f64(gain)[:, None] * np.tanh(lin + f64(b1)[:, None])
    h1 = h[:, unstriped(pos1)]
    h2 = h[:, unstriped(pos2)]
    hi = np.maximum(h1, h2)
    lo = np.minimum(h1, h2)
    top = mxq(f64(w2), 0, "e4m3").T @ mxq(hi, 0, "e4m3")
    low = unpack_weight(w3_words, w3_scales, "e2m1").T @ mxq(lo, 0, "e4m3")
    return np.square(top - low)

@@ -1,0 +1,266 @@
+from contextlib import ExitStack
+
+import concourse.mybir as mybir
+
+K, H, N, T, S, PAIRS = 1024, 1536, 384, 2048, 1024, 512
+FLOPS = 2 * K * H * S + 2 * 2 * H * N * PAIRS
+
+F32 = mybir.dt.float32
+BF16 = mybir.dt.bfloat16
+I32 = mybir.dt.int32
+U32 = mybir.dt.uint32
+U16 = mybir.dt.uint16
+U8 = mybir.dt.uint8
+FP8X4 = mybir.dt.float8_e4m3fn_x4
+FP4X4 = mybir.dt.float4_e2m1fn_x4
+ACT = mybir.ActivationFunctionType
+ALU = mybir.AluOpType
+
+P = 128
+PACK = 4
+K_PASS = P * PACK
+BANK = 512
+K_PASSES = K // K_PASS
+R_PASSES = H // K_PASS
+N_TILES = N // P
+VECTOR_SHARE = 80
+HALF = PAIRS // 2
+
+
+def tile_list_brew_pair_spread_kernel(
+    tc, tab_words, tab_scales, offs, w1, b1, gain, pos1, pos2, w2, w3_words, w3_scales, out
+):
+    nc = tc.nc
+    with ExitStack() as ctx:
+        keep = ctx.enter_context(tc.tile_pool(name="keep", bufs=1))
+        psum = ctx.enter_context(tc.psum_pool(name="psum", bufs=1))
+
+        offs_sb = keep.tile([P, S // 16], U16, name="offs_sb")
+        pos1_sb = keep.tile([P, PAIRS // 16], U16, name="pos1_sb")
+        pos2_sb = keep.tile([P, PAIRS // 16], U16, name="pos2_sb")
+        table_words = [keep.tile([P, T], U32, name="table_words%d" % a, align_bytes=64) for a in range(K_PASSES)]
+        table_bytes = keep.tile([P, T], U8, name="table_bytes")
+        picked_words = [keep.tile([P, S], U32, name="picked_words%d" % a, align_bytes=64) for a in range(K_PASSES)]
+        picked_bytes = keep.tile([P, S], U8, name="picked_bytes")
+        picked_plane = keep.tile([P, S], U8, name="picked_plane", align_bytes=64)
+        bias_sb = keep.tile([P, R_PASSES, PACK], F32, name="bias_sb")
+        gain_sb = keep.tile([P, R_PASSES, PACK], F32, name="gain_sb")
+        w3_plane = keep.tile([P, R_PASSES * N], U8, name="w3_plane", align_bytes=64)
+        warm = keep.tile([P, 2], F32, name="warm")
+        raw = [keep.tile([P, PACK * K_PASS], F32, name="raw%d" % u) for u in range(2)]
+        head_cast = [keep.tile([P, PACK * K_PASS], BF16, name="head_cast%d" % u, align_bytes=64) for u in range(2)]
+        bounded = [keep.tile([P, S], F32, name="bounded%d" % u) for u in range(2)]
+        h = [keep.tile([P, S], F32, name="h%d" % t, align_bytes=64) for t in range(PACK)]
+        first = keep.tile([P, PACK, PAIRS], F32, name="first")
+        second = keep.tile([P, PACK, PAIRS], F32, name="second")
+        pair_cast = keep.tile([P, 2 * PACK * PAIRS], BF16, name="pair_cast", align_bytes=64)
+        lo_cast = pair_cast[:, : PACK * PAIRS]
+        hi_cast = pair_cast[:, PACK * PAIRS :]
+        middle = pair_cast[:, PACK * PAIRS // 2 : 3 * PACK * PAIRS // 2]
+        banks = [psum.tile([P, BANK], F32, name="bank%d" % u) for u in range(8)]
+        diff = [[banks[4], banks[5], banks[6]], [banks[7], banks[0], banks[1]]]
+
+        nc.vector.memset(table_bytes[:].bitcast(I32), 0)
+        nc.vector.memset(warm[:, 0:1], 0.0)
+        nc.gpsimd.dma_start(bias_sb[:], b1.rearrange("(b p t) -> p b t", p=P, t=PACK))
+        nc.gpsimd.dma_start(gain_sb[:], gain.rearrange("(b p t) -> p b t", p=P, t=PACK))
+        nc.vector.memset(w3_plane[:].bitcast(I32), 0)
+        for d in range(4):
+            nc.gpsimd.dma_start(
+                w3_plane[:].bitcast(I32).rearrange("p (a n) -> p a n", a=R_PASSES)[32 * d : 32 * d + 4, :, :],
+                w3_scales[:, 4 * d : 4 * d + 4, :].rearrange("a q n -> q a n").bitcast(I32),
+            )
+        nc.scalar.activation(warm[:, 1:2], warm[:, 0:1], ACT.Tanh)
+
+        def load_table(a):
+            nc.sync.dma_start(table_words[a][:].bitcast(I32), tab_words[a].rearrange("p t i -> p (t i)").bitcast(I32))
+
+        def load_w1(b, a, dst):
+            rows = w1[a * K_PASS : (a + 1) * K_PASS, b * K_PASS : (b + 1) * K_PASS]
+            nc.sync.dma_start(dst[:].rearrange("p (j c) -> p j c", j=PACK), rows.rearrange("(p j) c -> p j c", j=PACK))
+
+        def load_w2(b, dst):
+            rows = w2[b * K_PASS : (b + 1) * K_PASS, :]
+            nc.sync.dma_start(dst[:, : PACK * N], rows.rearrange("(p j) n -> p (j n)", j=PACK))
+
+        def w1_views(dst, src, m0, m1):
+            return (
+                dst.rearrange("p (t m j) -> p m j t", t=PACK, j=PACK)[:, m0:m1, :, :],
+                src[:].rearrange("p (j m t) -> p m j t", j=PACK, t=PACK)[:, m0:m1, :, :],
+            )
+
+        def cast_w2(dst, src):
+            nc.scalar.activation(
+                dst.rearrange("p (c i j) -> p c j i", i=4, j=PACK),
+                src[:, : PACK * N].rearrange("p (j c i) -> p c j i", i=4, j=PACK),
+                ACT.Copy,
+                scale=-1.0,
+            )
+
+        def quantize(src, name, cuts):
+            width = src.shape[1] // PACK
+            codes = keep.tile([P, width], U32, name=name + "_codes", align_bytes=64)
+            plane = keep.tile([P, width], U8, name=name + "_plane", align_bytes=64)
+            for start, stop in zip(cuts[:-1], cuts[1:]):
+                nc.vector.quantize_mx(
+                    out=codes[:, start:stop].bitcast(FP8X4),
+                    scales=plane[:, start:stop],
+                    in_=src[:, PACK * start : PACK * stop],
+                )
+            return codes, plane
+
+        nc.sync.dma_start(offs_sb[:], offs)
+        load_table(0)
+        for a in range(K_PASSES):
+            nc.sync.dma_start(table_bytes[:].bitcast(I32)[4 * a : P : 8, :], tab_scales[a].bitcast(I32))
+        nc.sync.dma_start(pos1_sb[:], pos1)
+        nc.sync.dma_start(pos2_sb[:], pos2)
+        load_w1(0, 0, raw[0])
+        load_table(1)
+        load_w1(0, 1, raw[1])
+
+        nc.vector.tensor_copy(picked_bytes[:], table_bytes[:].indirect(offs_sb[:]))
+        nc.vector.tensor_copy(picked_plane[:].bitcast(I32), picked_bytes[:].bitcast(I32))
+        for a in range(K_PASSES):
+            for r in range(1, 4):
+                nc.scalar.dma_start(
+                    picked_plane[:].bitcast(I32)[4 * a + r : P : 32, :],
+                    picked_bytes[:].bitcast(I32)[4 * a + 8 * r : P : 32, :],
+                )
+        w1_mx = {}
+        w2_mx = {}
+        nc.vector.tensor_copy(picked_words[0][:], table_words[0][:].indirect(offs_sb[:]))
+        nc.scalar.copy(*w1_views(head_cast[0][:], raw[0], 0, P))
+        load_w1(1, 0, raw[0])
+        nc.vector.tensor_copy(picked_words[1][:], table_words[1][:].indirect(offs_sb[:]))
+        w1_mx[0, 0] = quantize(head_cast[0][:], "w1_00", (0, 512))
+        nc.vector.tensor_copy(*w1_views(head_cast[1][:], raw[1], 0, VECTOR_SHARE))
+        nc.scalar.copy(*w1_views(head_cast[1][:], raw[1], VECTOR_SHARE, P))
+        load_w1(1, 1, raw[1])
+        w1_mx[0, 1] = quantize(head_cast[1][:], "w1_01", (0, 128, 256, 512))
+        nc.vector.tensor_copy(*w1_views(head_cast[0][:], raw[0], 0, P))
+        load_w1(2, 0, raw[0])
+        w1_mx[1, 0] = quantize(head_cast[0][:], "w1_10", (0, 512))
+
+        w3_codes = keep.tile([P, R_PASSES * 2 * N], U8, name="w3_codes", tag="table_words1", align_bytes=64)
+        nc.sync.dma_start(
+            w3_codes[:].bitcast(I32).rearrange("p (a n) -> p a n", a=R_PASSES),
+            w3_words.rearrange("a p n -> p a n").bitcast(I32),
+        )
+
+        def features(b, t):
+            stage = middle.bitcast(F32) if t == PACK - 1 else bounded[t % 2][:]
+            for half in range(S // BANK):
+                cols = slice(half * BANK, (half + 1) * BANK)
+                lin = banks[2 * (t % 2) + half]
+                for a in range(K_PASSES):
+                    codes, plane = w1_mx[b, a]
+                    nc.tensor.matmul_mx(
+                        out=lin[:],
+                        lhsT=codes[:, t * P : (t + 1) * P].bitcast(FP8X4),
+                        lhsT_scale=plane[:, t * P : (t + 1) * P],
+                        rhs=picked_words[a][:, cols].bitcast(FP8X4),
+                        rhs_scale=picked_plane[4 * a : P, cols],
+                        start=(a == 0),
+                        stop=(a == K_PASSES - 1),
+                    )
+                nc.scalar.activation(stage[:, cols], lin[:], ACT.Tanh, bias=bias_sb[:, b, t : t + 1])
+                if b == 0 and t == 0:
+                    nc.vector.tensor_scalar(h[t][:, cols], stage[:, cols], gain_sb[:, b, t : t + 1], None, ALU.mult)
+            if b > 0 or t > 0:
+                nc.scalar.activation(h[t][:], stage, ACT.Copy, scale=gain_sb[:, b, t : t + 1])
+            nc.vector.tensor_copy(first[:, t, :], h[t][:].indirect(pos1_sb[:]))
+            nc.vector.tensor_copy(second[:, t, :], h[t][:].indirect(pos2_sb[:]))
+
+        def extreme(dst, op, pairs):
+            nc.vector.tensor_tensor(
+                dst.rearrange("p (c i t) -> p c t i", i=4, t=PACK),
+                first[:, :, pairs].rearrange("p t (c i) -> p c t i", i=4),
+                second[:, :, pairs].rearrange("p t (c i) -> p c t i", i=4),
+                op,
+            )
+
+        def low_reading(b, half, c):
+            col = b * N + c * P
+            for piece in range(HALF // P):
+                pairs = slice(half * HALF + piece * P, half * HALF + (piece + 1) * P)
+                nc.tensor.matmul_mx(
+                    out=diff[half][c][:, piece * P : (piece + 1) * P],
+                    lhsT=w3_codes[:, 2 * col : 2 * (col + P)].bitcast(FP4X4),
+                    lhsT_scale=w3_plane[:, col : col + P],
+                    rhs=lo_mx[b][0][:, pairs].bitcast(FP8X4),
+                    rhs_scale=lo_mx[b][1][:, pairs],
+                    start=(b == 0 and piece == 0),
+                    stop=False,
+                )
+
+        def top_reading(b, half, c):
+            pairs = slice(half * HALF, (half + 1) * HALF)
+            nc.tensor.matmul_mx(
+                out=diff[half][c][:, :HALF],
+                lhsT=w2_mx[b][0][:, c * P : (c + 1) * P].bitcast(FP8X4),
+                lhsT_scale=w2_mx[b][1][:, c * P : (c + 1) * P],
+                rhs=hi_mx[b][0][:, pairs].bitcast(FP8X4),
+                rhs_scale=hi_mx[b][1][:, pairs],
+                start=False,
+                stop=(b == R_PASSES - 1),
+            )
+
+        ALL = slice(0, PAIRS)
+        lo_mx = {}
+        W2_CUTS = (0, 256, N)
+        hi_mx = {}
+        for t in range(PACK):
+            features(0, t)
+        nc.scalar.copy(*w1_views(middle, raw[1], 0, P))
+        load_w1(2, 1, raw[1])
+        w1_mx[1, 1] = quantize(middle, "w1_11", (0, 512))
+        nc.scalar.copy(*w1_views(h[3][:].bitcast(BF16), raw[0], 0, P))
+        load_w2(0, raw[0])
+        extreme(lo_cast, ALU.min, ALL)
+        extreme(hi_cast, ALU.max, ALL)
+        lo_mx[0] = quantize(lo_cast, "lo0", (0, 512))
+        w1_mx[2, 0] = quantize(h[3][:].bitcast(BF16), "w1_20", (0, 512))
+        hi_mx[0] = quantize(hi_cast, "hi0", (0, 512))
+        for t in range(PACK):
+            features(1, t)
+        nc.scalar.copy(*w1_views(middle, raw[1], 0, P))
+        load_w2(1, raw[1])
+        w1_mx[2, 1] = quantize(middle, "w1_21", (0, 512))
+        w2_cast = [h[3 - b][:].bitcast(BF16)[:, : PACK * N] for b in range(2)]
+        cast_w2(w2_cast[0], raw[0])
+        load_w2(2, raw[0])
+        cast_w2(w2_cast[1], raw[1])
+        extreme(lo_cast, ALU.min, ALL)
+        extreme(hi_cast, ALU.max, ALL)
+        lo_mx[1] = quantize(lo_cast, "lo1", (0, 512))
+        w2_mx[0] = quantize(w2_cast[0], "w2_0", W2_CUTS)
+        hi_mx[1] = quantize(hi_cast, "hi1", (0, 512))
+        w2_mx[1] = quantize(w2_cast[1], "w2_1", W2_CUTS)
+        for t in range(PACK):
+            features(2, t)
+        for half in range(2):
+            for c in range(N_TILES):
+                for b in range(R_PASSES - 1):
+                    low_reading(b, half, c)
+                    top_reading(b, half, c)
+        cast_w2(head_cast[0][:, : PACK * N], raw[0])
+        extreme(lo_cast, ALU.min, ALL)
+        w2_mx[2] = quantize(head_cast[0][:, : PACK * N], "w2_2", W2_CUTS)
+        lo_mx[2] = quantize(lo_cast, "lo2", (0, 512))
+        for half in range(2):
+            extreme(lo_cast[:, half * PACK * HALF : (half + 1) * PACK * HALF], ALU.max, slice(half * HALF, (half + 1) * HALF))
+        for half in range(2):
+            for c in range(N_TILES):
+                low_reading(R_PASSES - 1, half, c)
+        hi_mx[2] = quantize(lo_cast, "hi2", (0, HALF, PAIRS))
+        result = keep.tile([P, 2, N_TILES, HALF], F32, name="result")
+        out_view = out.rearrange("(c p) m -> p c m", p=P)
+        for half in range(2):
+            for c in range(N_TILES):
+                top_reading(R_PASSES - 1, half, c)
+                nc.scalar.activation(result[:, half, c, :], diff[half][c][:, :HALF], ACT.Square)
+                if half == 1:
+                    nc.sync.dma_start(out_view[:, c, HALF:], result[:, half, c, :])
+            if half == 0:
+                nc.sync.dma_start(out_view[:, :, :HALF], result[:, half, :, :])

@@ -43,9 +43,9 @@ def tile_list_brew_pair_spread_kernel(
         picked_words = [keep.tile([P, S], U32, name="picked_words%d" % a, align_bytes=64) for a in range(K_PASSES)]
         picked_bytes = keep.tile([P, S], U8, name="picked_bytes")
         picked_plane = keep.tile([P, S], U8, name="picked_plane", align_bytes=64)
-        bias_sb = keep.tile([P, R_PASSES, PACK], F32, name="bias_sb")
-        gain_sb = keep.tile([P, R_PASSES, PACK], F32, name="gain_sb")
-        w3_plane = keep.tile([P, R_PASSES * N], U8, name="w3_plane", align_bytes=64)
+        bias_sb = keep.tile([P, R_PASSES, 2 * PACK], F32, name="bias_sb")
+        gain_sb = keep.tile([P, R_PASSES, 2 * PACK], F32, name="gain_sb")
+        early_planes = keep.tile([P, R_PASSES * K_PASS], U8, name="early_planes", align_bytes=64)
         warm = keep.tile([P, 2], F32, name="warm")
         raw = [keep.tile([P, PACK * K_PASS], F32, name="raw%d" % u) for u in range(2)]
         head_cast = [keep.tile([P, PACK * K_PASS], BF16, name="head_cast%d" % u, align_bytes=64) for u in range(2)]
@@ -56,24 +56,19 @@ def tile_list_brew_pair_spread_kernel(
         pair_cast = keep.tile([P, 2 * PACK * PAIRS], BF16, name="pair_cast", align_bytes=64)
         lo_cast = pair_cast[:, : PACK * PAIRS]
         hi_cast = pair_cast[:, PACK * PAIRS :]
-        middle = pair_cast[:, PACK * PAIRS // 2 : 3 * PACK * PAIRS // 2]
         banks = [psum.tile([P, BANK], F32, name="bank%d" % u) for u in range(8)]
-        diff = [[banks[4], banks[5], banks[6]], [banks[7], banks[0], banks[1]]]
+        diff = [banks[:N_TILES], banks[N_TILES : 2 * N_TILES]]
 
-        nc.vector.memset(table_bytes[:].bitcast(I32), 0)
+        nc.gpsimd.memset(table_bytes[:].bitcast(I32), 0)
         nc.vector.memset(warm[:, 0:1], 0.0)
-        nc.gpsimd.dma_start(bias_sb[:], b1.rearrange("(b p t) -> p b t", p=P, t=PACK))
-        nc.gpsimd.dma_start(gain_sb[:], gain.rearrange("(b p t) -> p b t", p=P, t=PACK))
-        nc.vector.memset(w3_plane[:].bitcast(I32), 0)
-        for d in range(4):
-            nc.gpsimd.dma_start(
-                w3_plane[:].bitcast(I32).rearrange("p (a n) -> p a n", a=R_PASSES)[32 * d : 32 * d + 4, :, :],
-                w3_scales[:, 4 * d : 4 * d + 4, :].rearrange("a q n -> q a n").bitcast(I32),
-            )
+        for blocks in (slice(0, 1), slice(1, R_PASSES)):
+            nc.gpsimd.dma_start(bias_sb[:, blocks, :PACK], b1.rearrange("(b p t) -> p b t", p=P, t=PACK)[:, blocks, :])
+            nc.gpsimd.dma_start(gain_sb[:, blocks, :PACK], gain.rearrange("(b p t) -> p b t", p=P, t=PACK)[:, blocks, :])
         nc.scalar.activation(warm[:, 1:2], warm[:, 0:1], ACT.Tanh)
 
-        def load_table(a):
-            nc.sync.dma_start(table_words[a][:].bitcast(I32), tab_words[a].rearrange("p t i -> p (t i)").bitcast(I32))
+        def load_table(a, start, stop):
+            words = tab_words[a].rearrange("p t i -> p (t i)").bitcast(I32)
+            nc.sync.dma_start(table_words[a][:].bitcast(I32)[:, start:stop], words[:, start:stop])
 
         def load_w1(b, a, dst):
             rows = w1[a * K_PASS : (a + 1) * K_PASS, b * K_PASS : (b + 1) * K_PASS]
@@ -97,26 +92,34 @@ def tile_list_brew_pair_spread_kernel(
                 scale=-1.0,
             )
 
-        def quantize(src, name, cuts):
-            width = src.shape[1] // PACK
+        def mx_tiles(name, width, plane=None):
             codes = keep.tile([P, width], U32, name=name + "_codes", align_bytes=64)
-            plane = keep.tile([P, width], U8, name=name + "_plane", align_bytes=64)
-            for start, stop in zip(cuts[:-1], cuts[1:]):
-                nc.vector.quantize_mx(
-                    out=codes[:, start:stop].bitcast(FP8X4),
-                    scales=plane[:, start:stop],
-                    in_=src[:, PACK * start : PACK * stop],
-                )
+            if plane is None:
+                plane = keep.tile([P, width], U8, name=name + "_plane", align_bytes=64)
             return codes, plane
 
+        def quantize_part(src, dst, start, stop):
+            nc.vector.quantize_mx(
+                out=dst[0][:, start:stop].bitcast(FP8X4),
+                scales=dst[1][:, start:stop],
+                in_=src[:, PACK * start : PACK * stop],
+            )
+
+        def quantize(src, name, cuts, plane=None):
+            dst = mx_tiles(name, src.shape[1] // PACK, plane)
+            for start, stop in zip(cuts[:-1], cuts[1:]):
+                quantize_part(src, dst, start, stop)
+            return dst
+
         nc.sync.dma_start(offs_sb[:], offs)
-        load_table(0)
+        load_table(0, 0, T // 2)
         for a in range(K_PASSES):
             nc.sync.dma_start(table_bytes[:].bitcast(I32)[4 * a : P : 8, :], tab_scales[a].bitcast(I32))
         nc.sync.dma_start(pos1_sb[:], pos1)
         nc.sync.dma_start(pos2_sb[:], pos2)
+        load_table(0, T // 2, T)
+        load_table(1, 0, T)
         load_w1(0, 0, raw[0])
-        load_table(1)
         load_w1(0, 1, raw[1])
 
         nc.vector.tensor_copy(picked_bytes[:], table_bytes[:].indirect(offs_sb[:]))
@@ -129,30 +132,35 @@ def tile_list_brew_pair_spread_kernel(
                 )
         w1_mx = {}
         w2_mx = {}
-        nc.vector.tensor_copy(picked_words[0][:], table_words[0][:].indirect(offs_sb[:]))
+        late_raw = []
+        for a in range(K_PASSES):
+            nc.vector.tensor_copy(picked_words[a][:], table_words[a][:].indirect(offs_sb[:]))
+            late_raw.append(keep.tile([P, PACK * K_PASS], F32, name="late_raw%d" % a, tag="table_words%d" % a, align_bytes=64))
+            load_w1(1, a, late_raw[a])
         nc.scalar.copy(*w1_views(head_cast[0][:], raw[0], 0, P))
-        load_w1(1, 0, raw[0])
-        nc.vector.tensor_copy(picked_words[1][:], table_words[1][:].indirect(offs_sb[:]))
-        w1_mx[0, 0] = quantize(head_cast[0][:], "w1_00", (0, 512))
+        load_w1(2, 0, raw[0])
         nc.vector.tensor_copy(*w1_views(head_cast[1][:], raw[1], 0, VECTOR_SHARE))
         nc.scalar.copy(*w1_views(head_cast[1][:], raw[1], VECTOR_SHARE, P))
-        load_w1(1, 1, raw[1])
-        w1_mx[0, 1] = quantize(head_cast[1][:], "w1_01", (0, 128, 256, 512))
-        nc.vector.tensor_copy(*w1_views(head_cast[0][:], raw[0], 0, P))
-        load_w1(2, 0, raw[0])
-        w1_mx[1, 0] = quantize(head_cast[0][:], "w1_10", (0, 512))
+        load_w1(2, 1, raw[1])
+        w1_mx[0, 0] = mx_tiles("w1_00", K_PASS, early_planes[:, :512])
+        w1_mx[0, 1] = mx_tiles("w1_01", K_PASS, early_planes[:, 512:1024])
+        for start, stop in ((0, 128), (128, 256), (256, 512)):
+            for a in range(K_PASSES):
+                quantize_part(head_cast[a][:], w1_mx[0, a], start, stop)
+        nc.vector.tensor_copy(*w1_views(head_cast[0][:], late_raw[0], 0, P))
+        w1_mx[1, 0] = quantize(head_cast[0][:], "w1_10", (0, 512), early_planes[:, 1024:])
 
-        w3_codes = keep.tile([P, R_PASSES * 2 * N], U8, name="w3_codes", tag="table_words1", align_bytes=64)
+        w3_codes = keep.tile([P, R_PASSES * 2 * N], U8, name="w3_codes", tag="head_cast1", align_bytes=64)
         nc.sync.dma_start(
             w3_codes[:].bitcast(I32).rearrange("p (a n) -> p a n", a=R_PASSES),
             w3_words.rearrange("a p n -> p a n").bitcast(I32),
         )
 
         def features(b, t):
-            stage = middle.bitcast(F32) if t == PACK - 1 else bounded[t % 2][:]
+            stage = hi_cast.bitcast(F32) if t == PACK - 1 else bounded[t % 2][:]
             for half in range(S // BANK):
                 cols = slice(half * BANK, (half + 1) * BANK)
-                lin = banks[2 * (t % 2) + half]
+                lin = banks[2 * t + half]
                 for a in range(K_PASSES):
                     codes, plane = w1_mx[b, a]
                     nc.tensor.matmul_mx(
@@ -165,7 +173,9 @@ def tile_list_brew_pair_spread_kernel(
                         stop=(a == K_PASSES - 1),
                     )
                 nc.scalar.activation(stage[:, cols], lin[:], ACT.Tanh, bias=bias_sb[:, b, t : t + 1])
-                if b == 0 and t == 0:
+                if b == 0 and t == 0 and half == 0:
+                    nc.scalar.activation(h[t][:, cols], stage[:, cols], ACT.Copy, scale=gain_sb[:, b, t : t + 1])
+                if b == 0 and t == 0 and half == 1:
                     nc.vector.tensor_scalar(h[t][:, cols], stage[:, cols], gain_sb[:, b, t : t + 1], None, ALU.mult)
             if b > 0 or t > 0:
                 nc.scalar.activation(h[t][:], stage, ACT.Copy, scale=gain_sb[:, b, t : t + 1])
@@ -187,7 +197,7 @@ def tile_list_brew_pair_spread_kernel(
                 nc.tensor.matmul_mx(
                     out=diff[half][c][:, piece * P : (piece + 1) * P],
                     lhsT=w3_codes[:, 2 * col : 2 * (col + P)].bitcast(FP4X4),
-                    lhsT_scale=w3_plane[:, col : col + P],
+                    lhsT_scale=early_planes[:, b * K_PASS + c * P : b * K_PASS + (c + 1) * P],
                     rhs=lo_mx[b][0][:, pairs].bitcast(FP8X4),
                     rhs_scale=lo_mx[b][1][:, pairs],
                     start=(b == 0 and piece == 0),
@@ -212,9 +222,8 @@ def tile_list_brew_pair_spread_kernel(
         hi_mx = {}
         for t in range(PACK):
             features(0, t)
-        nc.scalar.copy(*w1_views(middle, raw[1], 0, P))
-        load_w1(2, 1, raw[1])
-        w1_mx[1, 1] = quantize(middle, "w1_11", (0, 512))
+        nc.scalar.copy(*w1_views(hi_cast, late_raw[1], 0, P))
+        w1_mx[1, 1] = quantize(hi_cast, "w1_11", (0, 512))
         nc.scalar.copy(*w1_views(h[3][:].bitcast(BF16), raw[0], 0, P))
         load_w2(0, raw[0])
         extreme(lo_cast, ALU.min, ALL)
@@ -224,9 +233,14 @@ def tile_list_brew_pair_spread_kernel(
         hi_mx[0] = quantize(hi_cast, "hi0", (0, 512))
         for t in range(PACK):
             features(1, t)
-        nc.scalar.copy(*w1_views(middle, raw[1], 0, P))
+        for d in range(4):
+            nc.sync.dma_start(
+                early_planes[:].bitcast(I32).rearrange("p (a n) -> p a n", a=R_PASSES)[32 * d : 32 * d + 4, :, : N // 4],
+                w3_scales[:, 4 * d : 4 * d + 4, :].rearrange("a q n -> q a n").bitcast(I32),
+            )
+        nc.scalar.copy(*w1_views(hi_cast, raw[1], 0, P))
         load_w2(1, raw[1])
-        w1_mx[2, 1] = quantize(middle, "w1_21", (0, 512))
+        w1_mx[2, 1] = quantize(hi_cast, "w1_21", (0, 512))
         w2_cast = [h[3 - b][:].bitcast(BF16)[:, : PACK * N] for b in range(2)]
         cast_w2(w2_cast[0], raw[0])
         load_w2(2, raw[0])
@@ -247,16 +261,19 @@ def tile_list_brew_pair_spread_kernel(
         cast_w2(head_cast[0][:, : PACK * N], raw[0])
         extreme(lo_cast, ALU.min, ALL)
         w2_mx[2] = quantize(head_cast[0][:, : PACK * N], "w2_2", W2_CUTS)
-        lo_mx[2] = quantize(lo_cast, "lo2", (0, 512))
-        for half in range(2):
-            extreme(lo_cast[:, half * PACK * HALF : (half + 1) * PACK * HALF], ALU.max, slice(half * HALF, (half + 1) * HALF))
-        for half in range(2):
-            for c in range(N_TILES):
-                low_reading(R_PASSES - 1, half, c)
-        hi_mx[2] = quantize(lo_cast, "hi2", (0, HALF, PAIRS))
+        lo_mx[2] = mx_tiles("lo2", PAIRS)
+        hi_mx[2] = mx_tiles("hi2", PAIRS)
+        quantize_part(lo_cast, lo_mx[2], 0, HALF)
+        extreme(hi_cast[:, : PACK * HALF], ALU.max, slice(0, HALF))
+        quantize_part(lo_cast, lo_mx[2], HALF, PAIRS)
+        quantize_part(hi_cast, hi_mx[2], 0, HALF)
+        extreme(hi_cast[:, PACK * HALF :], ALU.max, slice(HALF, PAIRS))
+        quantize_part(hi_cast, hi_mx[2], HALF, PAIRS)
         result = keep.tile([P, 2, N_TILES, HALF], F32, name="result")
         out_view = out.rearrange("(c p) m -> p c m", p=P)
         for half in range(2):
+            for c in range(N_TILES):
+                low_reading(R_PASSES - 1, half, c)
             for c in range(N_TILES):
                 top_reading(R_PASSES - 1, half, c)
                 nc.scalar.activation(result[:, half, c, :], diff[half][c][:, :HALF], ACT.Square)

@@ -56,6 +56,7 @@ def tile_list_brew_pair_spread_kernel(
         pair_cast = keep.tile([P, 2 * PACK * PAIRS], BF16, name="pair_cast", align_bytes=64)
         lo_cast = pair_cast[:, : PACK * PAIRS]
         hi_cast = pair_cast[:, PACK * PAIRS :]
+        middle = pair_cast[:, PACK * PAIRS // 2 : 3 * PACK * PAIRS // 2]
         banks = [psum.tile([P, BANK], F32, name="bank%d" % u) for u in range(8)]
         diff = [banks[:N_TILES], banks[N_TILES : 2 * N_TILES]]
 
@@ -157,7 +158,7 @@ def tile_list_brew_pair_spread_kernel(
         )
 
         def features(b, t):
-            stage = hi_cast.bitcast(F32) if t == PACK - 1 else bounded[t % 2][:]
+            stage = middle.bitcast(F32) if t == PACK - 1 else bounded[t % 2][:]
             for half in range(S // BANK):
                 cols = slice(half * BANK, (half + 1) * BANK)
                 lin = banks[2 * t + half]
@@ -222,10 +223,12 @@ def tile_list_brew_pair_spread_kernel(
         hi_mx = {}
         for t in range(PACK):
             features(0, t)
-        nc.scalar.copy(*w1_views(hi_cast, late_raw[1], 0, P))
-        w1_mx[1, 1] = quantize(hi_cast, "w1_11", (0, 512))
+        nc.scalar.copy(*w1_views(middle, late_raw[1], 0, P))
+        w1_mx[1, 1] = quantize(middle, "w1_11", (0, 512))
         nc.scalar.copy(*w1_views(h[3][:].bitcast(BF16), raw[0], 0, P))
-        load_w2(0, raw[0])
+        load_w2(0, late_raw[0])
+        load_w2(1, late_raw[1])
+        load_w2(2, raw[0])
         extreme(lo_cast, ALU.min, ALL)
         extreme(hi_cast, ALU.max, ALL)
         lo_mx[0] = quantize(lo_cast, "lo0", (0, 512))
@@ -238,29 +241,28 @@ def tile_list_brew_pair_spread_kernel(
                 early_planes[:].bitcast(I32).rearrange("p (a n) -> p a n", a=R_PASSES)[32 * d : 32 * d + 4, :, : N // 4],
                 w3_scales[:, 4 * d : 4 * d + 4, :].rearrange("a q n -> q a n").bitcast(I32),
             )
-        nc.scalar.copy(*w1_views(hi_cast, raw[1], 0, P))
-        load_w2(1, raw[1])
-        w1_mx[2, 1] = quantize(hi_cast, "w1_21", (0, 512))
-        w2_cast = [h[3 - b][:].bitcast(BF16)[:, : PACK * N] for b in range(2)]
-        cast_w2(w2_cast[0], raw[0])
-        load_w2(2, raw[0])
-        cast_w2(w2_cast[1], raw[1])
+        nc.scalar.copy(*w1_views(middle, raw[1], 0, P))
+        w1_mx[2, 1] = quantize(middle, "w1_21", (0, 512))
+        w2_cast = [tile[:].bitcast(BF16)[:, : PACK * N] for tile in (h[3], bounded[1])]
+        cast_w2(w2_cast[0], late_raw[0])
         extreme(lo_cast, ALU.min, ALL)
         extreme(hi_cast, ALU.max, ALL)
         lo_mx[1] = quantize(lo_cast, "lo1", (0, 512))
         w2_mx[0] = quantize(w2_cast[0], "w2_0", W2_CUTS)
         hi_mx[1] = quantize(hi_cast, "hi1", (0, 512))
-        w2_mx[1] = quantize(w2_cast[1], "w2_1", W2_CUTS)
         for t in range(PACK):
             features(2, t)
-        for half in range(2):
-            for c in range(N_TILES):
-                for b in range(R_PASSES - 1):
-                    low_reading(b, half, c)
-                    top_reading(b, half, c)
-        cast_w2(head_cast[0][:, : PACK * N], raw[0])
-        extreme(lo_cast, ALU.min, ALL)
-        w2_mx[2] = quantize(head_cast[0][:, : PACK * N], "w2_2", W2_CUTS)
+        cast_w2(w2_cast[1], late_raw[1])
+        w2_mx[1] = quantize(w2_cast[1], "w2_1", W2_CUTS)
+        cast_w2(middle[:, : PACK * N], raw[0])
+        w2_mx[2] = quantize(middle[:, : PACK * N], "w2_2", W2_CUTS)
+        for b in range(R_PASSES - 1):
+            for reading in (low_reading, top_reading):
+                for half in range(2):
+                    for c in range(N_TILES):
+                        reading(b, half, c)
+        extreme(lo_cast[:, : PACK * HALF], ALU.min, slice(0, HALF))
+        extreme(lo_cast[:, PACK * HALF :], ALU.min, slice(HALF, PAIRS))
         lo_mx[2] = mx_tiles("lo2", PAIRS)
         hi_mx[2] = mx_tiles("hi2", PAIRS)
         quantize_part(lo_cast, lo_mx[2], 0, HALF)
@@ -274,10 +276,12 @@ def tile_list_brew_pair_spread_kernel(
         for half in range(2):
             for c in range(N_TILES):
                 low_reading(R_PASSES - 1, half, c)
+        for half in range(2):
             for c in range(N_TILES):
                 top_reading(R_PASSES - 1, half, c)
                 nc.scalar.activation(result[:, half, c, :], diff[half][c][:, :HALF], ACT.Square)
                 if half == 1:
-                    nc.sync.dma_start(out_view[:, c, HALF:], result[:, half, c, :])
+                    queue = nc.scalar if c == N_TILES - 1 else nc.sync
+                    queue.dma_start(out_view[:, c, HALF:], result[:, half, c, :])
             if half == 0:
                 nc.sync.dma_start(out_view[:, :, :HALF], result[:, half, :, :])

from contextlib import ExitStack

import concourse.mybir as mybir

K, H, N, T, S, PAIRS = 1024, 1536, 384, 2048, 1024, 512
FLOPS = 2 * K * H * S + 2 * 2 * H * N * PAIRS

F32 = mybir.dt.float32
BF16 = mybir.dt.bfloat16
I32 = mybir.dt.int32
U32 = mybir.dt.uint32
U16 = mybir.dt.uint16
U8 = mybir.dt.uint8
FP8X4 = mybir.dt.float8_e4m3fn_x4
FP4X4 = mybir.dt.float4_e2m1fn_x4
ACT = mybir.ActivationFunctionType
ALU = mybir.AluOpType

P = 128
PACK = 4
K_PASS = P * PACK
BANK = 512
K_PASSES = K // K_PASS
R_PASSES = H // K_PASS
N_TILES = N // P
VECTOR_SHARE = 80
HALF = PAIRS // 2


def tile_list_brew_pair_spread_kernel(
    tc, tab_words, tab_scales, offs, w1, b1, gain, pos1, pos2, w2, w3_words, w3_scales, out
):
    nc = tc.nc
    with ExitStack() as ctx:
        keep = ctx.enter_context(tc.tile_pool(name="keep", bufs=1))
        psum = ctx.enter_context(tc.psum_pool(name="psum", bufs=1))

        offs_sb = keep.tile([P, S // 16], U16, name="offs_sb")
        pos1_sb = keep.tile([P, PAIRS // 16], U16, name="pos1_sb")
        pos2_sb = keep.tile([P, PAIRS // 16], U16, name="pos2_sb")
        table_words = [keep.tile([P, T], U32, name="table_words%d" % a, align_bytes=64) for a in range(K_PASSES)]
        table_bytes = keep.tile([P, T], U8, name="table_bytes")
        picked_words = [keep.tile([P, S], U32, name="picked_words%d" % a, align_bytes=64) for a in range(K_PASSES)]
        picked_bytes = keep.tile([P, S], U8, name="picked_bytes")
        picked_plane = keep.tile([P, S], U8, name="picked_plane", align_bytes=64)
        bias_sb = keep.tile([P, R_PASSES, 2 * PACK], F32, name="bias_sb")
        gain_sb = keep.tile([P, R_PASSES, 2 * PACK], F32, name="gain_sb")
        early_planes = keep.tile([P, R_PASSES * K_PASS], U8, name="early_planes", align_bytes=64)
        warm = keep.tile([P, 2], F32, name="warm")
        raw = [keep.tile([P, PACK * K_PASS], F32, name="raw%d" % u) for u in range(2)]
        head_cast = [keep.tile([P, PACK * K_PASS], BF16, name="head_cast%d" % u, align_bytes=64) for u in range(2)]
        bounded = [keep.tile([P, S], F32, name="bounded%d" % u) for u in range(2)]
        h = [keep.tile([P, S], F32, name="h%d" % t, align_bytes=64) for t in range(PACK)]
        first = keep.tile([P, PACK, PAIRS], F32, name="first")
        second = keep.tile([P, PACK, PAIRS], F32, name="second")
        pair_cast = keep.tile([P, 2 * PACK * PAIRS], BF16, name="pair_cast", align_bytes=64)
        lo_cast = pair_cast[:, : PACK * PAIRS]
        hi_cast = pair_cast[:, PACK * PAIRS :]
        middle = pair_cast[:, PACK * PAIRS // 2 : 3 * PACK * PAIRS // 2]
        banks = [psum.tile([P, BANK], F32, name="bank%d" % u) for u in range(8)]
        diff = [banks[:N_TILES], banks[N_TILES : 2 * N_TILES]]

        nc.gpsimd.memset(table_bytes[:].bitcast(I32), 0)
        nc.vector.memset(warm[:, 0:1], 0.0)
        for blocks in (slice(0, 1), slice(1, R_PASSES)):
            nc.gpsimd.dma_start(bias_sb[:, blocks, :PACK], b1.rearrange("(b p t) -> p b t", p=P, t=PACK)[:, blocks, :])
            nc.gpsimd.dma_start(gain_sb[:, blocks, :PACK], gain.rearrange("(b p t) -> p b t", p=P, t=PACK)[:, blocks, :])
        nc.scalar.activation(warm[:, 1:2], warm[:, 0:1], ACT.Tanh)

        def load_table(a, start, stop):
            words = tab_words[a].rearrange("p t i -> p (t i)").bitcast(I32)
            nc.sync.dma_start(table_words[a][:].bitcast(I32)[:, start:stop], words[:, start:stop])

        def load_w1(b, a, dst):
            rows = w1[a * K_PASS : (a + 1) * K_PASS, b * K_PASS : (b + 1) * K_PASS]
            nc.sync.dma_start(dst[:].rearrange("p (j c) -> p j c", j=PACK), rows.rearrange("(p j) c -> p j c", j=PACK))

        def load_w2(b, dst):
            rows = w2[b * K_PASS : (b + 1) * K_PASS, :]
            nc.sync.dma_start(dst[:, : PACK * N], rows.rearrange("(p j) n -> p (j n)", j=PACK))

        def w1_views(dst, src, m0, m1):
            return (
                dst.rearrange("p (t m j) -> p m j t", t=PACK, j=PACK)[:, m0:m1, :, :],
                src[:].rearrange("p (j m t) -> p m j t", j=PACK, t=PACK)[:, m0:m1, :, :],
            )

        def cast_w2(dst, src):
            nc.scalar.activation(
                dst.rearrange("p (c i j) -> p c j i", i=4, j=PACK),
                src[:, : PACK * N].rearrange("p (j c i) -> p c j i", i=4, j=PACK),
                ACT.Copy,
                scale=-1.0,
            )

        def mx_tiles(name, width, plane=None):
            codes = keep.tile([P, width], U32, name=name + "_codes", align_bytes=64)
            if plane is None:
                plane = keep.tile([P, width], U8, name=name + "_plane", align_bytes=64)
            return codes, plane

        def quantize_part(src, dst, start, stop):
            nc.vector.quantize_mx(
                out=dst[0][:, start:stop].bitcast(FP8X4),
                scales=dst[1][:, start:stop],
                in_=src[:, PACK * start : PACK * stop],
            )

        def quantize(src, name, cuts, plane=None):
            dst = mx_tiles(name, src.shape[1] // PACK, plane)
            for start, stop in zip(cuts[:-1], cuts[1:]):
                quantize_part(src, dst, start, stop)
            return dst

        nc.sync.dma_start(offs_sb[:], offs)
        load_table(0, 0, T // 2)
        for a in range(K_PASSES):
            nc.sync.dma_start(table_bytes[:].bitcast(I32)[4 * a : P : 8, :], tab_scales[a].bitcast(I32))
        nc.sync.dma_start(pos1_sb[:], pos1)
        nc.sync.dma_start(pos2_sb[:], pos2)
        load_table(0, T // 2, T)
        load_table(1, 0, T)
        load_w1(0, 0, raw[0])
        load_w1(0, 1, raw[1])

        nc.vector.tensor_copy(picked_bytes[:], table_bytes[:].indirect(offs_sb[:]))
        nc.vector.tensor_copy(picked_plane[:].bitcast(I32), picked_bytes[:].bitcast(I32))
        for a in range(K_PASSES):
            for r in range(1, 4):
                nc.scalar.dma_start(
                    picked_plane[:].bitcast(I32)[4 * a + r : P : 32, :],
                    picked_bytes[:].bitcast(I32)[4 * a + 8 * r : P : 32, :],
                )
        w1_mx = {}
        w2_mx = {}
        late_raw = []
        for a in range(K_PASSES):
            nc.vector.tensor_copy(picked_words[a][:], table_words[a][:].indirect(offs_sb[:]))
            late_raw.append(keep.tile([P, PACK * K_PASS], F32, name="late_raw%d" % a, tag="table_words%d" % a, align_bytes=64))
            load_w1(1, a, late_raw[a])
        nc.scalar.copy(*w1_views(head_cast[0][:], raw[0], 0, P))
        load_w1(2, 0, raw[0])
        nc.vector.tensor_copy(*w1_views(head_cast[1][:], raw[1], 0, VECTOR_SHARE))
        nc.scalar.copy(*w1_views(head_cast[1][:], raw[1], VECTOR_SHARE, P))
        load_w1(2, 1, raw[1])
        w1_mx[0, 0] = mx_tiles("w1_00", K_PASS, early_planes[:, :512])
        w1_mx[0, 1] = mx_tiles("w1_01", K_PASS, early_planes[:, 512:1024])
        for start, stop in ((0, 128), (128, 256), (256, 512)):
            for a in range(K_PASSES):
                quantize_part(head_cast[a][:], w1_mx[0, a], start, stop)
        nc.vector.tensor_copy(*w1_views(head_cast[0][:], late_raw[0], 0, P))
        w1_mx[1, 0] = quantize(head_cast[0][:], "w1_10", (0, 512), early_planes[:, 1024:])

        w3_codes = keep.tile([P, R_PASSES * 2 * N], U8, name="w3_codes", tag="head_cast1", align_bytes=64)
        nc.sync.dma_start(
            w3_codes[:].bitcast(I32).rearrange("p (a n) -> p a n", a=R_PASSES),
            w3_words.rearrange("a p n -> p a n").bitcast(I32),
        )

        def features(b, t):
            stage = middle.bitcast(F32) if t == PACK - 1 else bounded[t % 2][:]
            for half in range(S // BANK):
                cols = slice(half * BANK, (half + 1) * BANK)
                lin = banks[2 * t + half]
                for a in range(K_PASSES):
                    codes, plane = w1_mx[b, a]
                    nc.tensor.matmul_mx(
                        out=lin[:],
                        lhsT=codes[:, t * P : (t + 1) * P].bitcast(FP8X4),
                        lhsT_scale=plane[:, t * P : (t + 1) * P],
                        rhs=picked_words[a][:, cols].bitcast(FP8X4),
                        rhs_scale=picked_plane[4 * a : P, cols],
                        start=(a == 0),
                        stop=(a == K_PASSES - 1),
                    )
                nc.scalar.activation(stage[:, cols], lin[:], ACT.Tanh, bias=bias_sb[:, b, t : t + 1])
                if b == 0 and t == 0 and half == 0:
                    nc.scalar.activation(h[t][:, cols], stage[:, cols], ACT.Copy, scale=gain_sb[:, b, t : t + 1])
                if b == 0 and t == 0 and half == 1:
                    nc.vector.tensor_scalar(h[t][:, cols], stage[:, cols], gain_sb[:, b, t : t + 1], None, ALU.mult)
            if b > 0 or t > 0:
                nc.scalar.activation(h[t][:], stage, ACT.Copy, scale=gain_sb[:, b, t : t + 1])
            nc.vector.tensor_copy(first[:, t, :], h[t][:].indirect(pos1_sb[:]))
            nc.vector.tensor_copy(second[:, t, :], h[t][:].indirect(pos2_sb[:]))

        def extreme(dst, op, pairs):
            nc.vector.tensor_tensor(
                dst.rearrange("p (c i t) -> p c t i", i=4, t=PACK),
                first[:, :, pairs].rearrange("p t (c i) -> p c t i", i=4),
                second[:, :, pairs].rearrange("p t (c i) -> p c t i", i=4),
                op,
            )

        def low_reading(b, half, c):
            col = b * N + c * P
            for piece in range(HALF // P):
                pairs = slice(half * HALF + piece * P, half * HALF + (piece + 1) * P)
                nc.tensor.matmul_mx(
                    out=diff[half][c][:, piece * P : (piece + 1) * P],
                    lhsT=w3_codes[:, 2 * col : 2 * (col + P)].bitcast(FP4X4),
                    lhsT_scale=early_planes[:, b * K_PASS + c * P : b * K_PASS + (c + 1) * P],
                    rhs=lo_mx[b][0][:, pairs].bitcast(FP8X4),
                    rhs_scale=lo_mx[b][1][:, pairs],
                    start=(b == 0 and piece == 0),
                    stop=False,
                )

        def top_reading(b, half, c):
            pairs = slice(half * HALF, (half + 1) * HALF)
            nc.tensor.matmul_mx(
                out=diff[half][c][:, :HALF],
                lhsT=w2_mx[b][0][:, c * P : (c + 1) * P].bitcast(FP8X4),
                lhsT_scale=w2_mx[b][1][:, c * P : (c + 1) * P],
                rhs=hi_mx[b][0][:, pairs].bitcast(FP8X4),
                rhs_scale=hi_mx[b][1][:, pairs],
                start=False,
                stop=(b == R_PASSES - 1),
            )

        ALL = slice(0, PAIRS)
        lo_mx = {}
        W2_CUTS = (0, 256, N)
        hi_mx = {}
        for t in range(PACK):
            features(0, t)
        nc.scalar.copy(*w1_views(middle, late_raw[1], 0, P))
        w1_mx[1, 1] = quantize(middle, "w1_11", (0, 512))
        nc.scalar.copy(*w1_views(h[3][:].bitcast(BF16), raw[0], 0, P))
        load_w2(0, late_raw[0])
        load_w2(1, late_raw[1])
        load_w2(2, raw[0])
        extreme(lo_cast, ALU.min, ALL)
        extreme(hi_cast, ALU.max, ALL)
        lo_mx[0] = quantize(lo_cast, "lo0", (0, 512))
        w1_mx[2, 0] = quantize(h[3][:].bitcast(BF16), "w1_20", (0, 512))
        hi_mx[0] = quantize(hi_cast, "hi0", (0, 512))
        for t in range(PACK):
            features(1, t)
        for d in range(4):
            nc.sync.dma_start(
                early_planes[:].bitcast(I32).rearrange("p (a n) -> p a n", a=R_PASSES)[32 * d : 32 * d + 4, :, : N // 4],
                w3_scales[:, 4 * d : 4 * d + 4, :].rearrange("a q n -> q a n").bitcast(I32),
            )
        nc.scalar.copy(*w1_views(middle, raw[1], 0, P))
        w1_mx[2, 1] = quantize(middle, "w1_21", (0, 512))
        w2_cast = [tile[:].bitcast(BF16)[:, : PACK * N] for tile in (h[3], bounded[1])]
        cast_w2(w2_cast[0], late_raw[0])
        extreme(lo_cast, ALU.min, ALL)
        extreme(hi_cast, ALU.max, ALL)
        lo_mx[1] = quantize(lo_cast, "lo1", (0, 512))
        w2_mx[0] = quantize(w2_cast[0], "w2_0", W2_CUTS)
        hi_mx[1] = quantize(hi_cast, "hi1", (0, 512))
        for t in range(PACK):
            features(2, t)
        cast_w2(w2_cast[1], late_raw[1])
        w2_mx[1] = quantize(w2_cast[1], "w2_1", W2_CUTS)
        cast_w2(middle[:, : PACK * N], raw[0])
        w2_mx[2] = quantize(middle[:, : PACK * N], "w2_2", W2_CUTS)
        for b in range(R_PASSES - 1):
            for reading in (low_reading, top_reading):
                for half in range(2):
                    for c in range(N_TILES):
                        reading(b, half, c)
        extreme(lo_cast[:, : PACK * HALF], ALU.min, slice(0, HALF))
        extreme(lo_cast[:, PACK * HALF :], ALU.min, slice(HALF, PAIRS))
        lo_mx[2] = mx_tiles("lo2", PAIRS)
        hi_mx[2] = mx_tiles("hi2", PAIRS)
        quantize_part(lo_cast, lo_mx[2], 0, HALF)
        extreme(hi_cast[:, : PACK * HALF], ALU.max, slice(0, HALF))
        quantize_part(lo_cast, lo_mx[2], HALF, PAIRS)
        quantize_part(hi_cast, hi_mx[2], 0, HALF)
        extreme(hi_cast[:, PACK * HALF :], ALU.max, slice(HALF, PAIRS))
        quantize_part(hi_cast, hi_mx[2], HALF, PAIRS)
        result = keep.tile([P, 2, N_TILES, HALF], F32, name="result")
        out_view = out.rearrange("(c p) m -> p c m", p=P)
        for half in range(2):
            for c in range(N_TILES):
                low_reading(R_PASSES - 1, half, c)
        for half in range(2):
            for c in range(N_TILES):
                top_reading(R_PASSES - 1, half, c)
                nc.scalar.activation(result[:, half, c, :], diff[half][c][:, :HALF], ACT.Square)
                if half == 1:
                    queue = nc.scalar if c == N_TILES - 1 else nc.sync
                    queue.dma_start(out_view[:, c, HALF:], result[:, half, c, :])
            if half == 0:
                nc.sync.dma_start(out_view[:, :, :HALF], result[:, half, :, :])
